import numpy as np
CORES = [0,1,2,3,4,5,6,7]
N = 8
ROUNDS = 4
def setup_inputs(rng):
    return {"x": rng.standard_normal((N, ROUNDS, 128, 512), dtype=np.float32)}
def reference(x):
    s = x.sum(axis=0, dtype=np.float64).astype(x.dtype)
    return {"y": np.broadcast_to(s, (N,) + s.shape)}

@@ -1,0 +1,70 @@
+from concourse.bass import DstId, RemoteDMATransfer
+from concourse.mybir import AluOpType
+
+N = 8
+PASSES = 2
+COLS = 512
+W = 2 * COLS // N
+
+SCRATCH = {
+    "xs": ("sbuf", [128, 2 * COLS], "float32"),
+    "land": ("sbuf", [128, N - 1, W], "float32"),
+}
+SEMAPHORES = ["local", "pieces", "sums", "left_s", "left_g"]
+
+
+def rank_program(g, core, T, topo):
+    r = T.rank_of(core)
+    if r is None:
+        return
+    xs, land, sem = T.xs, T.land, T.sem
+    others = [c for c in range(N) if c != r]
+
+    def dst_id(c):
+        rid, pid = topo.addr(T.cores[c])[:2]
+        return DstId(rid=rid, pnc=pid)
+
+    def chunk(c):
+        return xs[:, c * W:(c + 1) * W]
+
+    done = [0]
+
+    def local(out, in_, **kw):
+        g.dma_start(out, in_, **kw).then_inc(sem.local, 16)
+        done[0] += 16
+
+    def local_wait():
+        g.wait_ge(sem.local, done[0])
+
+    for p in range(PASSES):
+        local(xs[:, 0:COLS], T.x[2 * p])
+        local(xs[:, COLS:2 * COLS], T.x[2 * p + 1])
+        local_wait()
+
+        g.remote_dma_fused(
+            [RemoteDMATransfer(dst_ids=[dst_id(c)], dma_engine_mask=0x3 << (2 * i), remote_sem=sem.pieces,
+                               src=chunk(c), dst=land[:, (r - c) % N - 1, :])
+             for i, c in enumerate(others)],
+            local_sem=sem.left_s)
+        g.wait_ge(sem.pieces, 14 * (p + 1))
+
+        local(land[:, 0:3, :], land[:, 3:6, :], accum_op=AluOpType.add)
+        local_wait()
+        local(land[:, 0:2, :], land[:, 2:7:4, :], accum_op=AluOpType.add)
+        local_wait()
+        local(land[:, 0, :], land[:, 1, :], accum_op=AluOpType.add)
+        local_wait()
+        local(chunk(r), land[:, 0, :], accum_op=AluOpType.add)
+        local_wait()
+
+        g.remote_dma_fused(
+            [RemoteDMATransfer(dst_ids=[dst_id(c) for c in others], dma_engine_mask=0xFFFF, remote_sem=sem.sums,
+                               srcs=[chunk(r)], dsts=[chunk(r) for c in others])],
+            local_sem=sem.left_g)
+        g.wait_ge(sem.sums, 7 * 16 * (p + 1))
+
+        local(T.y[2 * p], xs[:, 0:COLS])
+        local(T.y[2 * p + 1], xs[:, COLS:2 * COLS])
+        local_wait()
+        g.wait_ge(sem.left_s, 14 * (p + 1))
+        g.wait_ge(sem.left_g, 16 * (p + 1))

@@ -3,12 +3,10 @@ from concourse.mybir import AluOpType
 
 N = 8
 PASSES = 2
-COLS = 512
-W = 2 * COLS // N
 
 SCRATCH = {
-    "xs": ("sbuf", [128, 2 * COLS], "float32"),
-    "land": ("sbuf", [128, N - 1, W], "float32"),
+    "xs": ("dram", [N, 128, 128], "float32"),
+    "land": ("dram", [N - 1, 128, 128], "float32"),
 }
 SEMAPHORES = ["local", "pieces", "sums", "left_s", "left_g"]
 
@@ -24,47 +22,45 @@ def rank_program(g, core, T, topo):
         rid, pid = topo.addr(T.cores[c])[:2]
         return DstId(rid=rid, pnc=pid)
 
-    def chunk(c):
-        return xs[:, c * W:(c + 1) * W]
-
     done = [0]
 
     def local(out, in_, **kw):
         g.dma_start(out, in_, **kw).then_inc(sem.local, 16)
         done[0] += 16
 
+    def add(out, in_):
+        local(out, in_, accum_op=AluOpType.add, max_dma_last_dim=8192)
+
     def local_wait():
         g.wait_ge(sem.local, done[0])
 
     for p in range(PASSES):
-        local(xs[:, 0:COLS], T.x[2 * p])
-        local(xs[:, COLS:2 * COLS], T.x[2 * p + 1])
+        local(xs[:], T.x[2 * p:2 * p + 2])
         local_wait()
 
         g.remote_dma_fused(
             [RemoteDMATransfer(dst_ids=[dst_id(c)], dma_engine_mask=0x3 << (2 * i), remote_sem=sem.pieces,
-                               src=chunk(c), dst=land[:, (r - c) % N - 1, :])
+                               src=xs[c], dst=land[(r - c) % N - 1])
              for i, c in enumerate(others)],
             local_sem=sem.left_s)
         g.wait_ge(sem.pieces, 14 * (p + 1))
 
-        local(land[:, 0:3, :], land[:, 3:6, :], accum_op=AluOpType.add)
+        add(land[0:3], land[3:6])
+        add(xs[r], land[6])
         local_wait()
-        local(land[:, 0:2, :], land[:, 2:7:4, :], accum_op=AluOpType.add)
+        add(land[0], land[1])
+        add(xs[r], land[2])
         local_wait()
-        local(land[:, 0, :], land[:, 1, :], accum_op=AluOpType.add)
-        local_wait()
-        local(chunk(r), land[:, 0, :], accum_op=AluOpType.add)
+        add(xs[r], land[0])
         local_wait()
 
         g.remote_dma_fused(
             [RemoteDMATransfer(dst_ids=[dst_id(c) for c in others], dma_engine_mask=0xFFFF, remote_sem=sem.sums,
-                               srcs=[chunk(r)], dsts=[chunk(r) for c in others])],
+                               srcs=[xs[r]], dsts=[xs[r] for c in others])],
             local_sem=sem.left_g)
         g.wait_ge(sem.sums, 7 * 16 * (p + 1))
 
-        local(T.y[2 * p], xs[:, 0:COLS])
-        local(T.y[2 * p + 1], xs[:, COLS:2 * COLS])
+        local(T.y[2 * p:2 * p + 2], xs[:])
         local_wait()
         g.wait_ge(sem.left_s, 14 * (p + 1))
         g.wait_ge(sem.left_g, 16 * (p + 1))

from concourse.bass import DstId, RemoteDMATransfer
from concourse.mybir import AluOpType

N = 8
PASSES = 2

SCRATCH = {
    "xs": ("dram", [N, 128, 128], "float32"),
    "land": ("dram", [N - 1, 128, 128], "float32"),
}
SEMAPHORES = ["local", "pieces", "sums", "left_s", "left_g"]


def rank_program(g, core, T, topo):
    r = T.rank_of(core)
    if r is None:
        return
    xs, land, sem = T.xs, T.land, T.sem
    others = [c for c in range(N) if c != r]

    def dst_id(c):
        rid, pid = topo.addr(T.cores[c])[:2]
        return DstId(rid=rid, pnc=pid)

    done = [0]

    def local(out, in_, **kw):
        g.dma_start(out, in_, **kw).then_inc(sem.local, 16)
        done[0] += 16

    def add(out, in_):
        local(out, in_, accum_op=AluOpType.add, max_dma_last_dim=8192)

    def local_wait():
        g.wait_ge(sem.local, done[0])

    for p in range(PASSES):
        local(xs[:], T.x[2 * p:2 * p + 2])
        local_wait()

        g.remote_dma_fused(
            [RemoteDMATransfer(dst_ids=[dst_id(c)], dma_engine_mask=0x3 << (2 * i), remote_sem=sem.pieces,
                               src=xs[c], dst=land[(r - c) % N - 1])
             for i, c in enumerate(others)],
            local_sem=sem.left_s)
        g.wait_ge(sem.pieces, 14 * (p + 1))

        add(land[0:3], land[3:6])
        add(xs[r], land[6])
        local_wait()
        add(land[0], land[1])
        add(xs[r], land[2])
        local_wait()
        add(xs[r], land[0])
        local_wait()

        g.remote_dma_fused(
            [RemoteDMATransfer(dst_ids=[dst_id(c) for c in others], dma_engine_mask=0xFFFF, remote_sem=sem.sums,
                               srcs=[xs[r]], dsts=[xs[r] for c in others])],
            local_sem=sem.left_g)
        g.wait_ge(sem.sums, 7 * 16 * (p + 1))

        local(T.y[2 * p:2 * p + 2], xs[:])
        local_wait()
        g.wait_ge(sem.left_s, 14 * (p + 1))
        g.wait_ge(sem.left_g, 16 * (p + 1))
